import numpy as np
import ml_dtypes


def mxq(x, axis, fmt="e4m3"):
    dtype, down = {"e4m3": (ml_dtypes.float8_e4m3fn, 7), "e5m2": (ml_dtypes.float8_e5m2, 14)}[fmt]
    v = np.moveaxis(np.asarray(x, np.float32).astype(ml_dtypes.bfloat16).astype(np.float64), axis, -1)
    blocks = v.reshape(v.shape[:-1] + (-1, 32))
    amax = np.abs(blocks).max(-1, keepdims=True)
    byte = np.maximum(np.where(amax > 0, np.frexp(amax)[1] - 1 + 127, 0) - down, 1)
    scale = np.exp2(byte - 127.0)
    codes = (blocks / scale).astype(np.float32).astype(dtype).astype(np.float64)
    return np.moveaxis((codes * scale).reshape(v.shape), -1, axis)


WIDE = False


def mx_kscale(k):
    if not WIDE:
        return np.ones(k)
    levels = np.array([10, -10, 5, -5, 0])
    if k % 512:
        return np.exp2(np.random.permutation(np.resize(levels, k // 32))).repeat(32)
    a = np.empty((k // 512, 16))
    for p in range(k // 512):
        a[p, :8] = np.random.permutation(np.resize(levels, 8))
        for g in range(8):
            far = levels[np.abs(levels - a[p, g]) >= 10]
            a[p, g + 8] = far[np.random.randint(len(far))]
    return np.exp2(a.ravel()).repeat(32)


def f64(x):
    return np.asarray(x).astype(np.float64)


def striped(idx):
    return np.tile(idx.reshape(-1, 16).T, (8, 1)).astype(np.uint16)


def unstriped(offs):
    return offs[:16].T.reshape(-1).astype(np.int64)


def pack_weight(w):
    k, n = w.shape
    w = f64(np.asarray(w, np.float32).astype(ml_dtypes.bfloat16)).reshape(k // 32, 32, n)
    amax = np.abs(w).max(1)
    byte = np.clip(np.where(amax > 0, np.frexp(amax)[1] - 1 + 127 - 7, 1), 1, 254)
    scaled = (w * np.exp2(127.0 - byte)[:, None, :]).reshape(k, n).astype(np.float32)
    words = np.ascontiguousarray(scaled.reshape(k // 512, 128, 4, n).transpose(0, 1, 3, 2)).astype(ml_dtypes.float8_e4m3fn).view(np.uint8)
    return words, np.ascontiguousarray(byte.astype(np.uint8).reshape(k // 512, 16, n))


def unpack_weight(words, scales):
    g, p, n, _ = words.shape
    vals = np.ascontiguousarray(words).view(ml_dtypes.float8_e4m3fn).astype(np.float64) * np.repeat(np.exp2(scales.astype(np.float64) - 127.0), 8, axis=1)[..., None]
    return vals.transpose(0, 1, 3, 2).reshape(g * 512, n)


def sigmoid(v):
    return 1.0 / (1.0 + np.exp(-np.maximum(v, -700.0)))


K, T, S, H, V, D, U = 1024, 2048, 512, 512, 256, 2, 512


def setup_inputs():
    n = np.random.standard_normal
    s = mx_kscale(K)[:, None]
    u = mx_kscale(H)
    packed_xT = pack_weight(n((K, T)) * s)
    return {
        "x_words": packed_xT[0],
        "x_scales": packed_xT[1],
        "w1": (n((K, H)) / np.sqrt(K) / s).astype(np.float32),
        "paq": (np.random.uniform(0.0, 1.0, (H, V)) ** 2 / H * 4 / u[:, None]).astype(np.float32),
        "unit": (np.random.uniform(0.7, 1.3, (H, 1)) * u[:, None]).astype(np.float32),
        "offs": striped(np.random.permutation(T)[:S]),
        "shown": striped(np.random.permutation(T)[:U]),
    }


def reference(x_words, x_scales, w1, paq, unit, offs, shown):
    x_shown = unpack_weight(x_words, x_scales)[:, unstriped(shown)]
    w1q = mxq(f64(w1), 0, "e4m3")
    ps = sigmoid((w1q.T @ x_shown) - 1.0)
    lg = np.log(-1.0 * ps + 1.001)
    nov = np.exp(lg.reshape(len(lg), -1, D).sum(axis=2))
    z = nov * f64(paq)
    xq = unpack_weight(x_words, x_scales)[:, unstriped(offs)]
    pd = sigmoid(w1q.T @ xq)
    dd = f64(unit) * pd
    return mxq(z, 0, "e4m3").T @ mxq(dd, 0, "e4m3")

@@ -1,0 +1,206 @@
+from contextlib import ExitStack
+
+import concourse.mybir as mybir
+
+K, T, S, H, V, U = 1024, 2048, 512, 512, 256, 512
+FLOPS = 2 * K * H * (S + U) + 2 * H * V * S
+
+F32 = mybir.dt.float32
+BF16 = mybir.dt.bfloat16
+I32 = mybir.dt.int32
+U32 = mybir.dt.uint32
+U16 = mybir.dt.uint16
+U8 = mybir.dt.uint8
+FP8X4 = mybir.dt.float8_e4m3fn_x4
+SIGMOID = mybir.ActivationFunctionType.Sigmoid
+ADD = mybir.AluOpType.add
+MULT = mybir.AluOpType.mult
+
+P = 128
+PACK = 4
+PASSES = K // (P * PACK)
+CAND_CHUNKS = ((0, 256), (256, 128), (384, 128))
+
+
+def tile_picked_yxquad_lin_p_kernel(tc, x_words, x_scales, w1, paq, unit, offs, shown, out):
+    nc = tc.nc
+    with ExitStack() as ctx:
+        keep = ctx.enter_context(tc.tile_pool(name="keep", bufs=1))
+        psum = ctx.enter_context(tc.psum_pool(name="psum", bufs=1))
+
+        def sb(name, shape, dtype):
+            return keep.tile(shape, dtype, name=name, align_bytes=64)
+
+        offs_t = keep.tile([P, S // 16], U16, name="offs_t")
+        shown_t = keep.tile([P, U // 16], U16, name="shown_t")
+        w_raw = [sb("w_raw%d" % g, [P, PACK, H], F32) for g in range(PASSES)]
+        x_tab = [sb("x_tab%d" % g, [P, T], I32) for g in range(PASSES)]
+        scale_tab = sb("scale_tab", [P, T], U8)
+        paq_raw = sb("paq_raw", [P, PACK, V], F32)
+        unit_t = sb("unit_t", [P, PACK], F32)
+
+        def load_w(g):
+            nc.sync.dma_start(out=w_raw[g][:], in_=w1[512 * g : 512 * (g + 1), :].rearrange("(p j) c -> p j c", j=PACK))
+
+        def load_x(g):
+            nc.sync.dma_start(out=x_tab[g][:], in_=x_words[g].rearrange("p n t -> p (n t)").bitcast(I32))
+
+        nc.vector.memset(scale_tab[:].bitcast(I32), 0)
+        load_w(0)
+        for q in range(4):
+            nc.sync.dma_start(
+                out=scale_tab[32 * q : 32 * q + 4 * PASSES, :].bitcast(I32),
+                in_=x_scales[:, 4 * q : 4 * q + 4, :].bitcast(I32),
+            )
+        nc.sync.dma_start(offs_t[:], offs)
+        nc.sync.dma_start(shown_t[:], shown)
+        load_x(0)
+        load_w(1)
+        load_x(1)
+        nc.sync.dma_start(out=paq_raw[:], in_=paq.rearrange("(p t) v -> p t v", t=PACK))
+        nc.sync.dma_start(out=unit_t[:], in_=unit.rearrange("(p t) o -> p (t o)", t=PACK))
+
+        warm = sb("warm", [P, 1], F32)
+        warm_out = sb("warm_out", [P, 1], F32)
+        nc.vector.memset(warm[:], 0.0)
+        nc.scalar.activation(out=warm_out[:], in_=warm[:], func=SIGMOID)
+
+        def gather(dst, table, offsets):
+            nc.vector.tensor_copy(out=dst, in_=table.indirect(offsets))
+
+        shown_scales = sb("shown_scales", [P, U], U8)
+        cand_scales = sb("cand_scales", [P, S], U8)
+        gather(shown_scales[:], scale_tab[:], shown_t[:])
+        gather(cand_scales[:], scale_tab[:], offs_t[:])
+
+        w_bf = [[sb("w_bf%d%d" % (g, hf), [P, 2, P, PACK], BF16) for hf in range(2)] for g in range(PASSES)]
+        w_codes = [[sb("w_codes%d%d" % (g, hf), [P, 2 * P], U32) for hf in range(2)] for g in range(PASSES)]
+        w_scales = [[sb("w_scales%d%d" % (g, hf), [P, 2 * P], U8) for hf in range(2)] for g in range(PASSES)]
+
+        def cast_w(g, hf, on_scalar):
+            src = w_raw[g][:].rearrange("p j (m t) -> p m j t", t=PACK)[:, :, :, 2 * hf : 2 * hf + 2]
+            dst = w_bf[g][hf][:].rearrange("p t m j -> p m j t")
+            if on_scalar:
+                nc.scalar.copy(out=dst, in_=src)
+            else:
+                nc.vector.tensor_copy(out=dst, in_=src)
+
+        def quantize(codes, scales, values):
+            nc.vector.quantize_mx(out=codes.bitcast(FP8X4), scales=scales, in_=values)
+
+        def quantize_w(g, hf):
+            quantize(w_codes[g][hf][:], w_scales[g][hf][:], w_bf[g][hf][:].rearrange("p t m j -> p (t m j)"))
+
+        def first_product(acc, g, t, words, scales):
+            cols = slice(P * (t % 2), P * (t % 2 + 1))
+            nc.tensor.matmul_mx(
+                out=acc,
+                lhsT=w_codes[g][t // 2][:, cols].bitcast(FP8X4),
+                lhsT_scale=w_scales[g][t // 2][:, cols],
+                rhs=words.bitcast(FP8X4),
+                rhs_scale=scales,
+                start=(g == 0),
+                stop=(g == PASSES - 1),
+            )
+
+        cast_w(0, 0, True)
+        cast_w(0, 1, True)
+        shown_words = [[sb("shown_words%d%d" % (g, hf), [P, 256], U32) for hf in range(2)] for g in range(PASSES)]
+        cand_words = [sb("cand_words%d" % g, [P, S], U32) for g in range(PASSES)]
+
+        def gather_shown(g, hf):
+            gather(shown_words[g][hf][:], x_tab[g][:].bitcast(U32), shown_t[:, 16 * hf : 16 * hf + 16])
+
+        def gather_cand(g):
+            gather(cand_words[g][:], x_tab[g][:].bitcast(U32), offs_t[:])
+
+        gather_cand(0)
+        quantize_w(0, 0)
+        quantize_w(0, 1)
+        gather_shown(0, 0)
+        gather_shown(0, 1)
+        cast_w(1, 0, True)
+        cast_w(1, 1, False)
+        quantize_w(1, 1)
+        quantize_w(1, 0)
+
+        cand_acc = [psum.tile([P, S], F32, name="cand_acc%d" % t) for t in range(PACK)]
+        for t in range(PACK):
+            first_product(cand_acc[t][:], 0, t, cand_words[0][:], cand_scales[:, :])
+
+        gather_shown(1, 0)
+        gather_shown(1, 1)
+        gather_cand(1)
+
+        uncovered = [sb("uncovered%d" % vt, [P, 2, P, PACK], F32) for vt in range(2)]
+        for b in range(4):
+            acc = psum.tile([P, PACK, P], F32, name="narrow", tag="narrow", bufs=4)
+            hf, part = divmod(b, 2)
+            for t in range(PACK):
+                for g in range(PASSES):
+                    first_product(
+                        acc[:, t, :], g, t,
+                        shown_words[g][hf][:, P * part : P * (part + 1)],
+                        shown_scales[4 * g :, P * b : P * (b + 1)],
+                    )
+            nc.scalar.activation(
+                out=uncovered[hf][:, :, 64 * part : 64 * (part + 1), :],
+                in_=acc[:].rearrange("p t (v d) -> p d v t", d=2),
+                func=SIGMOID, scale=-1.0, bias=1.0,
+            )
+
+        for t in range(PACK):
+            first_product(cand_acc[t][:], 1, t, cand_words[1][:], cand_scales[4:, :])
+
+        z_codes, z_scales = [], []
+        paq_w = [sb("paq_w%d" % vt, [P, P, PACK], F32) for vt in range(2)]
+        half_z = [sb("half_z%d" % vt, [P, P * PACK], F32) for vt in range(2)]
+        z_bf = [sb("z_bf%d" % vt, [P, P * PACK], BF16) for vt in range(2)]
+        for vt in range(2):
+            nc.vector.tensor_copy(
+                out=paq_w[vt][:].rearrange("p (c i) t -> p c t i", i=4),
+                in_=paq_raw[:, :, P * vt : P * (vt + 1)].rearrange("p t (c i) -> p c t i", i=4),
+            )
+        for vt in range(2):
+            nc.vector.scalar_tensor_tensor(
+                out=half_z[vt][:], in0=uncovered[vt][:, 0].rearrange("p v t -> p (v t)"), scalar=0.001,
+                in1=paq_w[vt][:].rearrange("p v t -> p (v t)"), op0=ADD, op1=MULT,
+            )
+        for vt in range(2):
+            nc.vector.scalar_tensor_tensor(
+                out=z_bf[vt][:], in0=uncovered[vt][:, 1].rearrange("p v t -> p (v t)"), scalar=0.001,
+                in1=half_z[vt][:], op0=ADD, op1=MULT,
+            )
+        for vt in range(2):
+            z_codes.append(sb("z_codes%d" % vt, [P, P], U32))
+            z_scales.append(sb("z_scales%d" % vt, [P, P], U8))
+            quantize(z_codes[vt][:], z_scales[vt][:], z_bf[vt][:])
+
+        out_view = out.rearrange("(vt p) j -> p vt j", p=P)
+        dd_bf = []
+        for c, (j0, n) in enumerate(CAND_CHUNKS):
+            covered = sb("covered%d" % c, [P, PACK, n], F32)
+            for t in range(PACK):
+                nc.scalar.activation(out=covered[:, t, :], in_=cand_acc[t][:, j0 : j0 + n], func=SIGMOID)
+            dd_bf.append(sb("dd_bf%d" % c, [P, n, PACK], BF16))
+            nc.vector.tensor_tensor(
+                out=dd_bf[c][:].rearrange("p (c i) t -> p c t i", i=4),
+                in0=covered[:].rearrange("p t (c i) -> p c t i", i=4),
+                in1=unit_t[:].unsqueeze(1).unsqueeze(3).to_broadcast([P, n // 4, PACK, 4]),
+                op=MULT,
+            )
+        for c, (j0, n) in enumerate(CAND_CHUNKS):
+            dd_codes = sb("dd_codes%d" % c, [P, n], U32)
+            dd_scales = sb("dd_scales%d" % c, [P, n], U8)
+            quantize(dd_codes[:], dd_scales[:], dd_bf[c][:].rearrange("p j t -> p (j t)"))
+            acc = psum.tile([P, 2, n], F32, name="scores", tag="narrow", bufs=4)
+            for vt in range(2):
+                nc.tensor.matmul_mx(
+                    out=acc[:, vt, :],
+                    lhsT=z_codes[vt][:].bitcast(FP8X4), lhsT_scale=z_scales[vt][:],
+                    rhs=dd_codes[:].bitcast(FP8X4), rhs_scale=dd_scales[:],
+                    start=True, stop=True,
+                )
+            result = sb("result%d" % c, [P, 2, n], F32)
+            nc.scalar.copy(out=result[:], in_=acc[:])
+            nc.sync.dma_start(out=out_view[:, :, j0 : j0 + n], in_=result[:])

@@ -13,6 +13,7 @@ U16 = mybir.dt.uint16
 U8 = mybir.dt.uint8
 FP8X4 = mybir.dt.float8_e4m3fn_x4
 SIGMOID = mybir.ActivationFunctionType.Sigmoid
+COPY = mybir.ActivationFunctionType.Copy
 ADD = mybir.AluOpType.add
 MULT = mybir.AluOpType.mult
 
@@ -28,15 +29,15 @@ def tile_picked_yxquad_lin_p_kernel(tc, x_words, x_scales, w1, paq, unit, offs, 
         keep = ctx.enter_context(tc.tile_pool(name="keep", bufs=1))
         psum = ctx.enter_context(tc.psum_pool(name="psum", bufs=1))
 
-        def sb(name, shape, dtype):
-            return keep.tile(shape, dtype, name=name, align_bytes=64)
+        def sb(name, shape, dtype, tag=""):
+            return keep.tile(shape, dtype, name=name, align_bytes=64, tag=tag)
 
         offs_t = keep.tile([P, S // 16], U16, name="offs_t")
         shown_t = keep.tile([P, U // 16], U16, name="shown_t")
         w_raw = [sb("w_raw%d" % g, [P, PACK, H], F32) for g in range(PASSES)]
-        x_tab = [sb("x_tab%d" % g, [P, T], I32) for g in range(PASSES)]
+        x_tab = [sb("x_tab%d" % g, [P, T], I32, tag="x_tab%d" % g) for g in range(PASSES)]
         scale_tab = sb("scale_tab", [P, T], U8)
-        paq_raw = sb("paq_raw", [P, PACK, V], F32)
+        paq_raw = [sb("paq_raw%d" % vt, [P, PACK, P], F32) for vt in range(2)]
         unit_t = sb("unit_t", [P, PACK], F32)
 
         def load_w(g):
@@ -45,20 +46,22 @@ def tile_picked_yxquad_lin_p_kernel(tc, x_words, x_scales, w1, paq, unit, offs, 
         def load_x(g):
             nc.sync.dma_start(out=x_tab[g][:], in_=x_words[g].rearrange("p n t -> p (n t)").bitcast(I32))
 
-        nc.vector.memset(scale_tab[:].bitcast(I32), 0)
+        load_x(0)
+        nc.sync.dma_start(offs_t[:], offs)
+        nc.sync.dma_start(shown_t[:], shown)
         load_w(0)
+        load_w(1)
+        load_x(1)
+        for vt in range(2):
+            nc.sync.dma_start(out=paq_raw[vt][:], in_=paq[:, P * vt : P * (vt + 1)].rearrange("(p t) v -> p t v", t=PACK))
+        nc.sync.dma_start(out=unit_t[:], in_=unit.rearrange("(p t) o -> p (t o)", t=PACK))
+
+        nc.gpsimd.memset(scale_tab[:].bitcast(I32), 0)
         for q in range(4):
-            nc.sync.dma_start(
+            nc.gpsimd.dma_start(
                 out=scale_tab[32 * q : 32 * q + 4 * PASSES, :].bitcast(I32),
                 in_=x_scales[:, 4 * q : 4 * q + 4, :].bitcast(I32),
             )
-        nc.sync.dma_start(offs_t[:], offs)
-        nc.sync.dma_start(shown_t[:], shown)
-        load_x(0)
-        load_w(1)
-        load_x(1)
-        nc.sync.dma_start(out=paq_raw[:], in_=paq.rearrange("(p t) v -> p t v", t=PACK))
-        nc.sync.dma_start(out=unit_t[:], in_=unit.rearrange("(p t) o -> p (t o)", t=PACK))
 
         warm = sb("warm", [P, 1], F32)
         warm_out = sb("warm_out", [P, 1], F32)
@@ -68,12 +71,7 @@ def tile_picked_yxquad_lin_p_kernel(tc, x_words, x_scales, w1, paq, unit, offs, 
         def gather(dst, table, offsets):
             nc.vector.tensor_copy(out=dst, in_=table.indirect(offsets))
 
-        shown_scales = sb("shown_scales", [P, U], U8)
-        cand_scales = sb("cand_scales", [P, S], U8)
-        gather(shown_scales[:], scale_tab[:], shown_t[:])
-        gather(cand_scales[:], scale_tab[:], offs_t[:])
-
-        w_bf = [[sb("w_bf%d%d" % (g, hf), [P, 2, P, PACK], BF16) for hf in range(2)] for g in range(PASSES)]
+        w_bf = [[sb("w_bf%d%d" % (g, hf), [P, 2, P, PACK], BF16, tag="w_bf%d%d" % (g, hf)) for hf in range(2)] for g in range(PASSES)]
         w_codes = [[sb("w_codes%d%d" % (g, hf), [P, 2 * P], U32) for hf in range(2)] for g in range(PASSES)]
         w_scales = [[sb("w_scales%d%d" % (g, hf), [P, 2 * P], U8) for hf in range(2)] for g in range(PASSES)]
 
@@ -105,32 +103,44 @@ def tile_picked_yxquad_lin_p_kernel(tc, x_words, x_scales, w1, paq, unit, offs, 
 
         cast_w(0, 0, True)
         cast_w(0, 1, True)
-        shown_words = [[sb("shown_words%d%d" % (g, hf), [P, 256], U32) for hf in range(2)] for g in range(PASSES)]
+        shown_first = sb("shown_first", [P, U], U32)
+        shown_last = [sb("shown_last%d" % hf, [P, 256], U32) for hf in range(2)]
+        shown_words = [[shown_first[:, :256], shown_first[:, 256:]], [shown_last[0][:], shown_last[1][:]]]
         cand_words = [sb("cand_words%d" % g, [P, S], U32) for g in range(PASSES)]
 
         def gather_shown(g, hf):
-            gather(shown_words[g][hf][:], x_tab[g][:].bitcast(U32), shown_t[:, 16 * hf : 16 * hf + 16])
+            gather(shown_words[g][hf], x_tab[g][:].bitcast(U32), shown_t[:, 16 * hf : 16 * hf + 16])
 
         def gather_cand(g):
             gather(cand_words[g][:], x_tab[g][:].bitcast(U32), offs_t[:])
 
         gather_cand(0)
+        gather(shown_first[:], x_tab[0][:].bitcast(U32), shown_t[:])
+        cand_scales = sb("cand_scales", [P, S], U8, tag="x_tab0")
+        gather(cand_scales[:], scale_tab[:], offs_t[:])
         quantize_w(0, 0)
-        quantize_w(0, 1)
-        gather_shown(0, 0)
-        gather_shown(0, 1)
+        shown_scales = sb("shown_scales", [P, U], U8, tag="w_bf00")
+        gather(shown_scales[:], scale_tab[:], shown_t[:])
         cast_w(1, 0, True)
+        quantize_w(0, 1)
         cast_w(1, 1, False)
-        quantize_w(1, 1)
         quantize_w(1, 0)
+        quantize_w(1, 1)
 
         cand_acc = [psum.tile([P, S], F32, name="cand_acc%d" % t) for t in range(PACK)]
         for t in range(PACK):
-            first_product(cand_acc[t][:], 0, t, cand_words[0][:], cand_scales[:, :])
+            first_product(cand_acc[t][:], 0, t, cand_words[0][:], cand_scales[:])
 
         gather_shown(1, 0)
         gather_shown(1, 1)
         gather_cand(1)
+
+        paq_w = [sb("paq_w%d" % vt, [P, P, PACK], F32) for vt in range(2)]
+        for vt, copy in enumerate((nc.scalar.copy, nc.vector.tensor_copy)):
+            copy(
+                out=paq_w[vt][:].rearrange("p (c i) t -> p c t i", i=4),
+                in_=paq_raw[vt][:].rearrange("p t (c i) -> p c t i", i=4),
+            )
 
         uncovered = [sb("uncovered%d" % vt, [P, 2, P, PACK], F32) for vt in range(2)]
         for b in range(4):
@@ -152,44 +162,47 @@ def tile_picked_yxquad_lin_p_kernel(tc, x_words, x_scales, w1, paq, unit, offs, 
         for t in range(PACK):
             first_product(cand_acc[t][:], 1, t, cand_words[1][:], cand_scales[4:, :])
 
-        z_codes, z_scales = [], []
-        paq_w = [sb("paq_w%d" % vt, [P, P, PACK], F32) for vt in range(2)]
         half_z = [sb("half_z%d" % vt, [P, P * PACK], F32) for vt in range(2)]
-        z_bf = [sb("z_bf%d" % vt, [P, P * PACK], BF16) for vt in range(2)]
-        for vt in range(2):
-            nc.vector.tensor_copy(
-                out=paq_w[vt][:].rearrange("p (c i) t -> p c t i", i=4),
-                in_=paq_raw[:, :, P * vt : P * (vt + 1)].rearrange("p t (c i) -> p c t i", i=4),
-            )
+        z_bf = sb("z_bf", [P, V * PACK], BF16)
+        z_codes = sb("z_codes", [P, V], U32)
+        z_scales = sb("z_scales", [P, V], U8)
         for vt in range(2):
             nc.vector.scalar_tensor_tensor(
                 out=half_z[vt][:], in0=uncovered[vt][:, 0].rearrange("p v t -> p (v t)"), scalar=0.001,
                 in1=paq_w[vt][:].rearrange("p v t -> p (v t)"), op0=ADD, op1=MULT,
             )
-        for vt in range(2):
             nc.vector.scalar_tensor_tensor(
-                out=z_bf[vt][:], in0=uncovered[vt][:, 1].rearrange("p v t -> p (v t)"), scalar=0.001,
+                out=z_bf[:, P * PACK * vt : P * PACK * (vt + 1)], in0=uncovered[vt][:, 1].rearrange("p v t -> p (v t)"), scalar=0.001,
                 in1=half_z[vt][:], op0=ADD, op1=MULT,
             )
-        for vt in range(2):
-            z_codes.append(sb("z_codes%d" % vt, [P, P], U32))
-            z_scales.append(sb("z_scales%d" % vt, [P, P], U8))
-            quantize(z_codes[vt][:], z_scales[vt][:], z_bf[vt][:])
 
         out_view = out.rearrange("(vt p) j -> p vt j", p=P)
-        dd_bf = []
-        for c, (j0, n) in enumerate(CAND_CHUNKS):
-            covered = sb("covered%d" % c, [P, PACK, n], F32)
+        dd_bf = [sb("dd_bf%d" % c, [P, n, PACK], BF16) for c, (j0, n) in enumerate(CAND_CHUNKS)]
+
+        covered = [sb("covered%d" % hf, [P, PACK, 256], F32) for hf in range(2)]
+        for hf in range(2):
             for t in range(PACK):
-                nc.scalar.activation(out=covered[:, t, :], in_=cand_acc[t][:, j0 : j0 + n], func=SIGMOID)
-            dd_bf.append(sb("dd_bf%d" % c, [P, n, PACK], BF16))
-            nc.vector.tensor_tensor(
-                out=dd_bf[c][:].rearrange("p (c i) t -> p c t i", i=4),
-                in0=covered[:].rearrange("p t (c i) -> p c t i", i=4),
-                in1=unit_t[:].unsqueeze(1).unsqueeze(3).to_broadcast([P, n // 4, PACK, 4]),
-                op=MULT,
-            )
-        for c, (j0, n) in enumerate(CAND_CHUNKS):
+                nc.scalar.activation(out=covered[hf][:, t, :], in_=cand_acc[t][:, 256 * hf : 256 * (hf + 1)], func=SIGMOID)
+
+        def make_dd(c):
+            j0, n = CAND_CHUNKS[c]
+            values = covered[j0 // 256][:, :, j0 % 256 : j0 % 256 + n]
+            dst = dd_bf[c][:].rearrange("p (c i) t -> p c t i", i=4)
+            if c == len(CAND_CHUNKS) - 1:
+                planes = sb("planes", [P, PACK, n], BF16)
+                for t in range(PACK):
+                    nc.scalar.activation(out=planes[:, t, :], in_=values[:, t, :], func=COPY, scale=unit_t[:, t : t + 1])
+                nc.scalar.copy(out=dst, in_=planes[:].rearrange("p t (c i) -> p c t i", i=4))
+            else:
+                nc.vector.tensor_tensor(
+                    out=dst,
+                    in0=values.rearrange("p t (c i) -> p c t i", i=4),
+                    in1=unit_t[:].unsqueeze(1).unsqueeze(3).to_broadcast([P, n // 4, PACK, 4]),
+                    op=MULT,
+                )
+
+        def score(c):
+            j0, n = CAND_CHUNKS[c]
             dd_codes = sb("dd_codes%d" % c, [P, n], U32)
             dd_scales = sb("dd_scales%d" % c, [P, n], U8)
             quantize(dd_codes[:], dd_scales[:], dd_bf[c][:].rearrange("p j t -> p (j t)"))
@@ -197,10 +210,21 @@ def tile_picked_yxquad_lin_p_kernel(tc, x_words, x_scales, w1, paq, unit, offs, 
             for vt in range(2):
                 nc.tensor.matmul_mx(
                     out=acc[:, vt, :],
-                    lhsT=z_codes[vt][:].bitcast(FP8X4), lhsT_scale=z_scales[vt][:],
+                    lhsT=z_codes[:, P * vt : P * (vt + 1)].bitcast(FP8X4), lhsT_scale=z_scales[:, P * vt : P * (vt + 1)],
                     rhs=dd_codes[:].bitcast(FP8X4), rhs_scale=dd_scales[:],
                     start=True, stop=True,
                 )
             result = sb("result%d" % c, [P, 2, n], F32)
-            nc.scalar.copy(out=result[:], in_=acc[:])
+            if c == 1:
+                nc.vector.tensor_copy(out=result[:], in_=acc[:])
+            else:
+                nc.scalar.copy(out=result[:], in_=acc[:])
             nc.sync.dma_start(out=out_view[:, :, j0 : j0 + n], in_=result[:])
+
+        make_dd(0)
+        make_dd(2)
+        quantize(z_codes[:], z_scales[:], z_bf[:])
+        score(0)
+        make_dd(1)
+        score(2)
+        score(1)

@@ -20,6 +20,7 @@ MULT = mybir.AluOpType.mult
 P = 128
 PACK = 4
 PASSES = K // (P * PACK)
+SCALAR_M = 80
 CAND_CHUNKS = ((0, 256), (256, 128), (384, 128))
 
 
@@ -46,22 +47,21 @@ def tile_picked_yxquad_lin_p_kernel(tc, x_words, x_scales, w1, paq, unit, offs, 
         def load_x(g):
             nc.sync.dma_start(out=x_tab[g][:], in_=x_words[g].rearrange("p n t -> p (n t)").bitcast(I32))
 
+        nc.vector.memset(scale_tab[:].bitcast(I32), 0)
         load_x(0)
         nc.sync.dma_start(offs_t[:], offs)
         nc.sync.dma_start(shown_t[:], shown)
+        for q in range(4):
+            nc.sync.dma_start(
+                out=scale_tab[32 * q : 32 * q + 4 * PASSES, :].bitcast(I32),
+                in_=x_scales[:, 4 * q : 4 * q + 4, :].bitcast(I32),
+            )
         load_w(0)
         load_w(1)
         load_x(1)
         for vt in range(2):
             nc.sync.dma_start(out=paq_raw[vt][:], in_=paq[:, P * vt : P * (vt + 1)].rearrange("(p t) v -> p t v", t=PACK))
         nc.sync.dma_start(out=unit_t[:], in_=unit.rearrange("(p t) o -> p (t o)", t=PACK))
-
-        nc.gpsimd.memset(scale_tab[:].bitcast(I32), 0)
-        for q in range(4):
-            nc.gpsimd.dma_start(
-                out=scale_tab[32 * q : 32 * q + 4 * PASSES, :].bitcast(I32),
-                in_=x_scales[:, 4 * q : 4 * q + 4, :].bitcast(I32),
-            )
 
         warm = sb("warm", [P, 1], F32)
         warm_out = sb("warm_out", [P, 1], F32)
@@ -71,38 +71,35 @@ def tile_picked_yxquad_lin_p_kernel(tc, x_words, x_scales, w1, paq, unit, offs, 
         def gather(dst, table, offsets):
             nc.vector.tensor_copy(out=dst, in_=table.indirect(offsets))
 
-        w_bf = [[sb("w_bf%d%d" % (g, hf), [P, 2, P, PACK], BF16, tag="w_bf%d%d" % (g, hf)) for hf in range(2)] for g in range(PASSES)]
-        w_codes = [[sb("w_codes%d%d" % (g, hf), [P, 2 * P], U32) for hf in range(2)] for g in range(PASSES)]
-        w_scales = [[sb("w_scales%d%d" % (g, hf), [P, 2 * P], U8) for hf in range(2)] for g in range(PASSES)]
+        w_bf_first = [sb("w_bf0%d" % hf, [P, 2, P, PACK], BF16, tag="w_bf0%d" % hf) for hf in range(2)]
+        w_bf_last = sb("w_bf1", [P, PACK, P, PACK], BF16)
+        w_codes = [sb("w_codes%d" % g, [P, H], U32) for g in range(PASSES)]
+        w_scales = [sb("w_scales%d" % g, [P, H], U8) for g in range(PASSES)]
 
-        def cast_w(g, hf, on_scalar):
-            src = w_raw[g][:].rearrange("p j (m t) -> p m j t", t=PACK)[:, :, :, 2 * hf : 2 * hf + 2]
-            dst = w_bf[g][hf][:].rearrange("p t m j -> p m j t")
-            if on_scalar:
-                nc.scalar.copy(out=dst, in_=src)
-            else:
-                nc.vector.tensor_copy(out=dst, in_=src)
+        def cast_w(copy, g, dst, ms, ts):
+            src = w_raw[g][:].rearrange("p j (m t) -> p m j t", t=PACK)[:, ms, :, ts]
+            copy(out=dst.rearrange("p t m j -> p m j t")[:, ms], in_=src)
 
         def quantize(codes, scales, values):
             nc.vector.quantize_mx(out=codes.bitcast(FP8X4), scales=scales, in_=values)
 
-        def quantize_w(g, hf):
-            quantize(w_codes[g][hf][:], w_scales[g][hf][:], w_bf[g][hf][:].rearrange("p t m j -> p (t m j)"))
+        def quantize_w(g, cols, values):
+            quantize(w_codes[g][:, cols], w_scales[g][:, cols], values.rearrange("p t m j -> p (t m j)"))
 
         def first_product(acc, g, t, words, scales):
-            cols = slice(P * (t % 2), P * (t % 2 + 1))
+            cols = slice(P * t, P * (t + 1))
             nc.tensor.matmul_mx(
                 out=acc,
-                lhsT=w_codes[g][t // 2][:, cols].bitcast(FP8X4),
-                lhsT_scale=w_scales[g][t // 2][:, cols],
+                lhsT=w_codes[g][:, cols].bitcast(FP8X4),
+                lhsT_scale=w_scales[g][:, cols],
                 rhs=words.bitcast(FP8X4),
                 rhs_scale=scales,
                 start=(g == 0),
                 stop=(g == PASSES - 1),
             )
 
-        cast_w(0, 0, True)
-        cast_w(0, 1, True)
+        for hf in range(2):
+            cast_w(nc.scalar.copy, 0, w_bf_first[hf][:], slice(0, P), slice(2 * hf, 2 * hf + 2))
         shown_first = sb("shown_first", [P, U], U32)
         shown_last = [sb("shown_last%d" % hf, [P, 256], U32) for hf in range(2)]
         shown_words = [[shown_first[:, :256], shown_first[:, 256:]], [shown_last[0][:], shown_last[1][:]]]
@@ -118,14 +115,13 @@ def tile_picked_yxquad_lin_p_kernel(tc, x_words, x_scales, w1, paq, unit, offs, 
         gather(shown_first[:], x_tab[0][:].bitcast(U32), shown_t[:])
         cand_scales = sb("cand_scales", [P, S], U8, tag="x_tab0")
         gather(cand_scales[:], scale_tab[:], offs_t[:])
-        quantize_w(0, 0)
+        quantize_w(0, slice(0, 2 * P), w_bf_first[0][:])
         shown_scales = sb("shown_scales", [P, U], U8, tag="w_bf00")
         gather(shown_scales[:], scale_tab[:], shown_t[:])
-        cast_w(1, 0, True)
-        quantize_w(0, 1)
-        cast_w(1, 1, False)
-        quantize_w(1, 0)
-        quantize_w(1, 1)
+        cast_w(nc.scalar.copy, 1, w_bf_last[:], slice(0, SCALAR_M), slice(0, PACK))
+        cast_w(nc.vector.tensor_copy, 1, w_bf_last[:], slice(SCALAR_M, P), slice(0, PACK))
+        quantize_w(0, slice(2 * P, H), w_bf_first[1][:])
+        quantize_w(1, slice(0, H), w_bf_last[:])
 
         cand_acc = [psum.tile([P, S], F32, name="cand_acc%d" % t) for t in range(PACK)]
         for t in range(PACK):
@@ -166,15 +162,18 @@ def tile_picked_yxquad_lin_p_kernel(tc, x_words, x_scales, w1, paq, unit, offs, 
         z_bf = sb("z_bf", [P, V * PACK], BF16)
         z_codes = sb("z_codes", [P, V], U32)
         z_scales = sb("z_scales", [P, V], U8)
+        def piece(flat, x):
+            return flat.rearrange("p (bank x c) -> p bank x c", bank=2, x=2)[:, :, x, :]
+
         for vt in range(2):
-            nc.vector.scalar_tensor_tensor(
-                out=half_z[vt][:], in0=uncovered[vt][:, 0].rearrange("p v t -> p (v t)"), scalar=0.001,
-                in1=paq_w[vt][:].rearrange("p v t -> p (v t)"), op0=ADD, op1=MULT,
-            )
-            nc.vector.scalar_tensor_tensor(
-                out=z_bf[:, P * PACK * vt : P * PACK * (vt + 1)], in0=uncovered[vt][:, 1].rearrange("p v t -> p (v t)"), scalar=0.001,
-                in1=half_z[vt][:], op0=ADD, op1=MULT,
-            )
+            factors = (paq_w[vt][:].rearrange("p v t -> p (v t)"), half_z[vt][:])
+            products = (half_z[vt][:], z_bf[:, P * PACK * vt : P * PACK * (vt + 1)])
+            for d in range(2):
+                for x in range(2):
+                    nc.vector.scalar_tensor_tensor(
+                        out=piece(products[d], x), in0=piece(uncovered[vt][:, d].rearrange("p v t -> p (v t)"), x), scalar=0.001,
+                        in1=piece(factors[d], x), op0=ADD, op1=MULT,
+                    )
 
         out_view = out.rearrange("(vt p) j -> p vt j", p=P)
         dd_bf = [sb("dd_bf%d" % c, [P, n, PACK], BF16) for c, (j0, n) in enumerate(CAND_CHUNKS)]
@@ -189,7 +188,7 @@ def tile_picked_yxquad_lin_p_kernel(tc, x_words, x_scales, w1, paq, unit, offs, 
             values = covered[j0 // 256][:, :, j0 % 256 : j0 % 256 + n]
             dst = dd_bf[c][:].rearrange("p (c i) t -> p c t i", i=4)
             if c == len(CAND_CHUNKS) - 1:
-                planes = sb("planes", [P, PACK, n], BF16)
+                planes = sb("planes", [P, PACK, n], BF16, tag="planes")
                 for t in range(PACK):
                     nc.scalar.activation(out=planes[:, t, :], in_=values[:, t, :], func=COPY, scale=unit_t[:, t : t + 1])
                 nc.scalar.copy(out=dst, in_=planes[:].rearrange("p t (c i) -> p c t i", i=4))
@@ -214,7 +213,7 @@ def tile_picked_yxquad_lin_p_kernel(tc, x_words, x_scales, w1, paq, unit, offs, 
                     rhs=dd_codes[:].bitcast(FP8X4), rhs_scale=dd_scales[:],
                     start=True, stop=True,
                 )
-            result = sb("result%d" % c, [P, 2, n], F32)
+            result = sb("result%d" % c, [P, 2, n], F32, tag="planes" if c == 0 else "")
             if c == 1:
                 nc.vector.tensor_copy(out=result[:], in_=acc[:])
             else:

@@ -20,7 +20,7 @@ MULT = mybir.AluOpType.mult
 P = 128
 PACK = 4
 PASSES = K // (P * PACK)
-SCALAR_M = 80
+SCALAR_M = (72, 48)
 CAND_CHUNKS = ((0, 256), (256, 128), (384, 128))
 
 
@@ -35,11 +35,9 @@ def tile_picked_yxquad_lin_p_kernel(tc, x_words, x_scales, w1, paq, unit, offs, 
 
         offs_t = keep.tile([P, S // 16], U16, name="offs_t")
         shown_t = keep.tile([P, U // 16], U16, name="shown_t")
-        w_raw = [sb("w_raw%d" % g, [P, PACK, H], F32) for g in range(PASSES)]
-        x_tab = [sb("x_tab%d" % g, [P, T], I32, tag="x_tab%d" % g) for g in range(PASSES)]
-        scale_tab = sb("scale_tab", [P, T], U8)
-        paq_raw = [sb("paq_raw%d" % vt, [P, PACK, P], F32) for vt in range(2)]
-        unit_t = sb("unit_t", [P, PACK], F32)
+        w_raw = [sb("w_raw%d" % g, [P, PACK, H], F32, tag="w_raw%d" % g) for g in range(PASSES)]
+        x_tab = [sb("x_tab0", [P, T], I32)]
+        scale_tab = sb("scale_tab", [P, T], U8, tag="table")
 
         def load_w(g):
             nc.sync.dma_start(out=w_raw[g][:], in_=w1[512 * g : 512 * (g + 1), :].rearrange("(p j) c -> p j c", j=PACK))
@@ -47,21 +45,19 @@ def tile_picked_yxquad_lin_p_kernel(tc, x_words, x_scales, w1, paq, unit, offs, 
         def load_x(g):
             nc.sync.dma_start(out=x_tab[g][:], in_=x_words[g].rearrange("p n t -> p (n t)").bitcast(I32))
 
-        nc.vector.memset(scale_tab[:].bitcast(I32), 0)
-        load_x(0)
+        nc.sync.dma_start(
+            out=scale_tab[0:32, :].bitcast(I32),
+            in_=x_scales.rearrange("o row n -> row o n").bitcast(I32),
+        )
         nc.sync.dma_start(offs_t[:], offs)
         nc.sync.dma_start(shown_t[:], shown)
-        for q in range(4):
-            nc.sync.dma_start(
-                out=scale_tab[32 * q : 32 * q + 4 * PASSES, :].bitcast(I32),
-                in_=x_scales[:, 4 * q : 4 * q + 4, :].bitcast(I32),
-            )
+        load_x(0)
         load_w(0)
         load_w(1)
-        load_x(1)
-        for vt in range(2):
-            nc.sync.dma_start(out=paq_raw[vt][:], in_=paq[:, P * vt : P * (vt + 1)].rearrange("(p t) v -> p t v", t=PACK))
-        nc.sync.dma_start(out=unit_t[:], in_=unit.rearrange("(p t) o -> p (t o)", t=PACK))
+        nc.vector.memset(scale_tab[32:64, :].bitcast(I32), 0)
+        nc.vector.memset(scale_tab[64:128, :].bitcast(I32), 0)
+        placed = sb("placed", [P, PASSES, S + U], U8)
+        nc.gpsimd.memset(placed[:].rearrange("p o n -> p (o n)").bitcast(I32), 0)
 
         warm = sb("warm", [P, 1], F32)
         warm_out = sb("warm_out", [P, 1], F32)
@@ -71,20 +67,32 @@ def tile_picked_yxquad_lin_p_kernel(tc, x_words, x_scales, w1, paq, unit, offs, 
         def gather(dst, table, offsets):
             nc.vector.tensor_copy(out=dst, in_=table.indirect(offsets))
 
-        w_bf_first = [sb("w_bf0%d" % hf, [P, 2, P, PACK], BF16, tag="w_bf0%d" % hf) for hf in range(2)]
-        w_bf_last = sb("w_bf1", [P, PACK, P, PACK], BF16)
+        picked = sb("picked", [P, S + U], U8)
+        gather(picked[:, :S], scale_tab[:], offs_t[:])
+        gather(picked[:, S:], scale_tab[:], shown_t[:])
+        for q in range(4):
+            nc.sync.dma_start(
+                out=placed[32 * q : 32 * q + 4].rearrange("p o n -> p (o n)").bitcast(I32),
+                in_=picked[8 * q : 8 * q + 8, :].bitcast(I32),
+            )
+        x_tab.append(sb("x_tab1", [P, T], I32, tag="table"))
+        load_x(1)
+
+        w_bf = [sb("w_bf%d" % g, [P, PACK, P, PACK], BF16) for g in range(PASSES)]
         w_codes = [sb("w_codes%d" % g, [P, H], U32) for g in range(PASSES)]
         w_scales = [sb("w_scales%d" % g, [P, H], U8) for g in range(PASSES)]
 
-        def cast_w(copy, g, dst, ms, ts):
-            src = w_raw[g][:].rearrange("p j (m t) -> p m j t", t=PACK)[:, ms, :, ts]
-            copy(out=dst.rearrange("p t m j -> p m j t")[:, ms], in_=src)
+        def cast_w(g):
+            src = w_raw[g][:].rearrange("p j (m t) -> p m j t", t=PACK)
+            dst = w_bf[g][:].rearrange("p t m j -> p m j t")
+            nc.scalar.copy(out=dst[:, : SCALAR_M[g]], in_=src[:, : SCALAR_M[g]])
+            nc.vector.tensor_copy(out=dst[:, SCALAR_M[g] :], in_=src[:, SCALAR_M[g] :])
 
         def quantize(codes, scales, values):
             nc.vector.quantize_mx(out=codes.bitcast(FP8X4), scales=scales, in_=values)
 
-        def quantize_w(g, cols, values):
-            quantize(w_codes[g][:, cols], w_scales[g][:, cols], values.rearrange("p t m j -> p (t m j)"))
+        def quantize_w(g):
+            quantize(w_codes[g][:], w_scales[g][:], w_bf[g][:].rearrange("p t m j -> p (t m j)"))
 
         def first_product(acc, g, t, words, scales):
             cols = slice(P * t, P * (t + 1))
@@ -98,8 +106,6 @@ def tile_picked_yxquad_lin_p_kernel(tc, x_words, x_scales, w1, paq, unit, offs, 
                 stop=(g == PASSES - 1),
             )
 
-        for hf in range(2):
-            cast_w(nc.scalar.copy, 0, w_bf_first[hf][:], slice(0, P), slice(2 * hf, 2 * hf + 2))
         shown_first = sb("shown_first", [P, U], U32)
         shown_last = [sb("shown_last%d" % hf, [P, 256], U32) for hf in range(2)]
         shown_words = [[shown_first[:, :256], shown_first[:, 256:]], [shown_last[0][:], shown_last[1][:]]]
@@ -113,19 +119,20 @@ def tile_picked_yxquad_lin_p_kernel(tc, x_words, x_scales, w1, paq, unit, offs, 
 
         gather_cand(0)
         gather(shown_first[:], x_tab[0][:].bitcast(U32), shown_t[:])
-        cand_scales = sb("cand_scales", [P, S], U8, tag="x_tab0")
-        gather(cand_scales[:], scale_tab[:], offs_t[:])
-        quantize_w(0, slice(0, 2 * P), w_bf_first[0][:])
-        shown_scales = sb("shown_scales", [P, U], U8, tag="w_bf00")
-        gather(shown_scales[:], scale_tab[:], shown_t[:])
-        cast_w(nc.scalar.copy, 1, w_bf_last[:], slice(0, SCALAR_M), slice(0, PACK))
-        cast_w(nc.vector.tensor_copy, 1, w_bf_last[:], slice(SCALAR_M, P), slice(0, PACK))
-        quantize_w(0, slice(2 * P, H), w_bf_first[1][:])
-        quantize_w(1, slice(0, H), w_bf_last[:])
+        cast_w(0)
+        quantize_w(0)
+        late = sb("late", [P, V * PACK + PACK], F32, tag="w_raw0")
+        paq_raw = [late[:, P * PACK * vt : P * PACK * (vt + 1)].rearrange("p (t v) -> p t v", t=PACK) for vt in range(2)]
+        unit_t = late[:, V * PACK :]
+        for vt in range(2):
+            nc.sync.dma_start(out=paq_raw[vt], in_=paq[:, P * vt : P * (vt + 1)].rearrange("(p t) v -> p t v", t=PACK))
+        nc.sync.dma_start(out=unit_t, in_=unit.rearrange("(p t) o -> p (t o)", t=PACK))
+        cast_w(1)
+        quantize_w(1)
 
         cand_acc = [psum.tile([P, S], F32, name="cand_acc%d" % t) for t in range(PACK)]
         for t in range(PACK):
-            first_product(cand_acc[t][:], 0, t, cand_words[0][:], cand_scales[:])
+            first_product(cand_acc[t][:], 0, t, cand_words[0][:], placed[:, 0, :S])
 
         gather_shown(1, 0)
         gather_shown(1, 1)
@@ -135,7 +142,7 @@ def tile_picked_yxquad_lin_p_kernel(tc, x_words, x_scales, w1, paq, unit, offs, 
         for vt, copy in enumerate((nc.scalar.copy, nc.vector.tensor_copy)):
             copy(
                 out=paq_w[vt][:].rearrange("p (c i) t -> p c t i", i=4),
-                in_=paq_raw[vt][:].rearrange("p t (c i) -> p c t i", i=4),
+                in_=paq_raw[vt].rearrange("p t (c i) -> p c t i", i=4),
             )
 
         uncovered = [sb("uncovered%d" % vt, [P, 2, P, PACK], F32) for vt in range(2)]
@@ -147,7 +154,7 @@ def tile_picked_yxquad_lin_p_kernel(tc, x_words, x_scales, w1, paq, unit, offs, 
                     first_product(
                         acc[:, t, :], g, t,
                         shown_words[g][hf][:, P * part : P * (part + 1)],
-                        shown_scales[4 * g :, P * b : P * (b + 1)],
+                        placed[:, g, S + P * b : S + P * (b + 1)],
                     )
             nc.scalar.activation(
                 out=uncovered[hf][:, :, 64 * part : 64 * (part + 1), :],
@@ -156,7 +163,7 @@ def tile_picked_yxquad_lin_p_kernel(tc, x_words, x_scales, w1, paq, unit, offs, 
             )
 
         for t in range(PACK):
-            first_product(cand_acc[t][:], 1, t, cand_words[1][:], cand_scales[4:, :])
+            first_product(cand_acc[t][:], 1, t, cand_words[1][:], placed[:, 1, :S])
 
         half_z = [sb("half_z%d" % vt, [P, P * PACK], F32) for vt in range(2)]
         z_bf = sb("z_bf", [P, V * PACK], BF16)
@@ -196,7 +203,7 @@ def tile_picked_yxquad_lin_p_kernel(tc, x_words, x_scales, w1, paq, unit, offs, 
                 nc.vector.tensor_tensor(
                     out=dst,
                     in0=values.rearrange("p t (c i) -> p c t i", i=4),
-                    in1=unit_t[:].unsqueeze(1).unsqueeze(3).to_broadcast([P, n // 4, PACK, 4]),
+                    in1=unit_t.unsqueeze(1).unsqueeze(3).to_broadcast([P, n // 4, PACK, 4]),
                     op=MULT,
                 )
 

@@ -20,7 +20,6 @@ MULT = mybir.AluOpType.mult
 P = 128
 PACK = 4
 PASSES = K // (P * PACK)
-SCALAR_M = (72, 48)
 CAND_CHUNKS = ((0, 256), (256, 128), (384, 128))
 
 
@@ -59,11 +58,6 @@ def tile_picked_yxquad_lin_p_kernel(tc, x_words, x_scales, w1, paq, unit, offs, 
         placed = sb("placed", [P, PASSES, S + U], U8)
         nc.gpsimd.memset(placed[:].rearrange("p o n -> p (o n)").bitcast(I32), 0)
 
-        warm = sb("warm", [P, 1], F32)
-        warm_out = sb("warm_out", [P, 1], F32)
-        nc.vector.memset(warm[:], 0.0)
-        nc.scalar.activation(out=warm_out[:], in_=warm[:], func=SIGMOID)
-
         def gather(dst, table, offsets):
             nc.vector.tensor_copy(out=dst, in_=table.indirect(offsets))
 
@@ -85,8 +79,7 @@ def tile_picked_yxquad_lin_p_kernel(tc, x_words, x_scales, w1, paq, unit, offs, 
         def cast_w(g):
             src = w_raw[g][:].rearrange("p j (m t) -> p m j t", t=PACK)
             dst = w_bf[g][:].rearrange("p t m j -> p m j t")
-            nc.scalar.copy(out=dst[:, : SCALAR_M[g]], in_=src[:, : SCALAR_M[g]])
-            nc.vector.tensor_copy(out=dst[:, SCALAR_M[g] :], in_=src[:, SCALAR_M[g] :])
+            nc.vector.tensor_copy(out=dst, in_=src)
 
         def quantize(codes, scales, values):
             nc.vector.quantize_mx(out=codes.bitcast(FP8X4), scales=scales, in_=values)
@@ -139,8 +132,8 @@ def tile_picked_yxquad_lin_p_kernel(tc, x_words, x_scales, w1, paq, unit, offs, 
         gather_cand(1)
 
         paq_w = [sb("paq_w%d" % vt, [P, P, PACK], F32) for vt in range(2)]
-        for vt, copy in enumerate((nc.scalar.copy, nc.vector.tensor_copy)):
-            copy(
+        for vt in range(2):
+            nc.vector.tensor_copy(
                 out=paq_w[vt][:].rearrange("p (c i) t -> p c t i", i=4),
                 in_=paq_raw[vt].rearrange("p t (c i) -> p c t i", i=4),
             )
@@ -232,5 +225,5 @@ def tile_picked_yxquad_lin_p_kernel(tc, x_words, x_scales, w1, paq, unit, offs, 
         quantize(z_codes[:], z_scales[:], z_bf[:])
         score(0)
         make_dd(1)
-        score(2)
         score(1)
+        score(2)

from contextlib import ExitStack

import concourse.mybir as mybir

K, T, S, H, V, U = 1024, 2048, 512, 512, 256, 512
FLOPS = 2 * K * H * (S + U) + 2 * H * V * S

F32 = mybir.dt.float32
BF16 = mybir.dt.bfloat16
I32 = mybir.dt.int32
U32 = mybir.dt.uint32
U16 = mybir.dt.uint16
U8 = mybir.dt.uint8
FP8X4 = mybir.dt.float8_e4m3fn_x4
SIGMOID = mybir.ActivationFunctionType.Sigmoid
COPY = mybir.ActivationFunctionType.Copy
ADD = mybir.AluOpType.add
MULT = mybir.AluOpType.mult

P = 128
PACK = 4
PASSES = K // (P * PACK)
CAND_CHUNKS = ((0, 256), (256, 128), (384, 128))


def tile_picked_yxquad_lin_p_kernel(tc, x_words, x_scales, w1, paq, unit, offs, shown, out):
    nc = tc.nc
    with ExitStack() as ctx:
        keep = ctx.enter_context(tc.tile_pool(name="keep", bufs=1))
        psum = ctx.enter_context(tc.psum_pool(name="psum", bufs=1))

        def sb(name, shape, dtype, tag=""):
            return keep.tile(shape, dtype, name=name, align_bytes=64, tag=tag)

        offs_t = keep.tile([P, S // 16], U16, name="offs_t")
        shown_t = keep.tile([P, U // 16], U16, name="shown_t")
        w_raw = [sb("w_raw%d" % g, [P, PACK, H], F32, tag="w_raw%d" % g) for g in range(PASSES)]
        x_tab = [sb("x_tab0", [P, T], I32)]
        scale_tab = sb("scale_tab", [P, T], U8, tag="table")

        def load_w(g):
            nc.sync.dma_start(out=w_raw[g][:], in_=w1[512 * g : 512 * (g + 1), :].rearrange("(p j) c -> p j c", j=PACK))

        def load_x(g):
            nc.sync.dma_start(out=x_tab[g][:], in_=x_words[g].rearrange("p n t -> p (n t)").bitcast(I32))

        nc.sync.dma_start(
            out=scale_tab[0:32, :].bitcast(I32),
            in_=x_scales.rearrange("o row n -> row o n").bitcast(I32),
        )
        nc.sync.dma_start(offs_t[:], offs)
        nc.sync.dma_start(shown_t[:], shown)
        load_x(0)
        load_w(0)
        load_w(1)
        nc.vector.memset(scale_tab[32:64, :].bitcast(I32), 0)
        nc.vector.memset(scale_tab[64:128, :].bitcast(I32), 0)
        placed = sb("placed", [P, PASSES, S + U], U8)
        nc.gpsimd.memset(placed[:].rearrange("p o n -> p (o n)").bitcast(I32), 0)

        def gather(dst, table, offsets):
            nc.vector.tensor_copy(out=dst, in_=table.indirect(offsets))

        picked = sb("picked", [P, S + U], U8)
        gather(picked[:, :S], scale_tab[:], offs_t[:])
        gather(picked[:, S:], scale_tab[:], shown_t[:])
        for q in range(4):
            nc.sync.dma_start(
                out=placed[32 * q : 32 * q + 4].rearrange("p o n -> p (o n)").bitcast(I32),
                in_=picked[8 * q : 8 * q + 8, :].bitcast(I32),
            )
        x_tab.append(sb("x_tab1", [P, T], I32, tag="table"))
        load_x(1)

        w_bf = [sb("w_bf%d" % g, [P, PACK, P, PACK], BF16) for g in range(PASSES)]
        w_codes = [sb("w_codes%d" % g, [P, H], U32) for g in range(PASSES)]
        w_scales = [sb("w_scales%d" % g, [P, H], U8) for g in range(PASSES)]

        def cast_w(g):
            src = w_raw[g][:].rearrange("p j (m t) -> p m j t", t=PACK)
            dst = w_bf[g][:].rearrange("p t m j -> p m j t")
            nc.vector.tensor_copy(out=dst, in_=src)

        def quantize(codes, scales, values):
            nc.vector.quantize_mx(out=codes.bitcast(FP8X4), scales=scales, in_=values)

        def quantize_w(g):
            quantize(w_codes[g][:], w_scales[g][:], w_bf[g][:].rearrange("p t m j -> p (t m j)"))

        def first_product(acc, g, t, words, scales):
            cols = slice(P * t, P * (t + 1))
            nc.tensor.matmul_mx(
                out=acc,
                lhsT=w_codes[g][:, cols].bitcast(FP8X4),
                lhsT_scale=w_scales[g][:, cols],
                rhs=words.bitcast(FP8X4),
                rhs_scale=scales,
                start=(g == 0),
                stop=(g == PASSES - 1),
            )

        shown_first = sb("shown_first", [P, U], U32)
        shown_last = [sb("shown_last%d" % hf, [P, 256], U32) for hf in range(2)]
        shown_words = [[shown_first[:, :256], shown_first[:, 256:]], [shown_last[0][:], shown_last[1][:]]]
        cand_words = [sb("cand_words%d" % g, [P, S], U32) for g in range(PASSES)]

        def gather_shown(g, hf):
            gather(shown_words[g][hf], x_tab[g][:].bitcast(U32), shown_t[:, 16 * hf : 16 * hf + 16])

        def gather_cand(g):
            gather(cand_words[g][:], x_tab[g][:].bitcast(U32), offs_t[:])

        gather_cand(0)
        gather(shown_first[:], x_tab[0][:].bitcast(U32), shown_t[:])
        cast_w(0)
        quantize_w(0)
        late = sb("late", [P, V * PACK + PACK], F32, tag="w_raw0")
        paq_raw = [late[:, P * PACK * vt : P * PACK * (vt + 1)].rearrange("p (t v) -> p t v", t=PACK) for vt in range(2)]
        unit_t = late[:, V * PACK :]
        for vt in range(2):
            nc.sync.dma_start(out=paq_raw[vt], in_=paq[:, P * vt : P * (vt + 1)].rearrange("(p t) v -> p t v", t=PACK))
        nc.sync.dma_start(out=unit_t, in_=unit.rearrange("(p t) o -> p (t o)", t=PACK))
        cast_w(1)
        quantize_w(1)

        cand_acc = [psum.tile([P, S], F32, name="cand_acc%d" % t) for t in range(PACK)]
        for t in range(PACK):
            first_product(cand_acc[t][:], 0, t, cand_words[0][:], placed[:, 0, :S])

        gather_shown(1, 0)
        gather_shown(1, 1)
        gather_cand(1)

        paq_w = [sb("paq_w%d" % vt, [P, P, PACK], F32) for vt in range(2)]
        for vt in range(2):
            nc.vector.tensor_copy(
                out=paq_w[vt][:].rearrange("p (c i) t -> p c t i", i=4),
                in_=paq_raw[vt].rearrange("p t (c i) -> p c t i", i=4),
            )

        uncovered = [sb("uncovered%d" % vt, [P, 2, P, PACK], F32) for vt in range(2)]
        for b in range(4):
            acc = psum.tile([P, PACK, P], F32, name="narrow", tag="narrow", bufs=4)
            hf, part = divmod(b, 2)
            for t in range(PACK):
                for g in range(PASSES):
                    first_product(
                        acc[:, t, :], g, t,
                        shown_words[g][hf][:, P * part : P * (part + 1)],
                        placed[:, g, S + P * b : S + P * (b + 1)],
                    )
            nc.scalar.activation(
                out=uncovered[hf][:, :, 64 * part : 64 * (part + 1), :],
                in_=acc[:].rearrange("p t (v d) -> p d v t", d=2),
                func=SIGMOID, scale=-1.0, bias=1.0,
            )

        for t in range(PACK):
            first_product(cand_acc[t][:], 1, t, cand_words[1][:], placed[:, 1, :S])

        half_z = [sb("half_z%d" % vt, [P, P * PACK], F32) for vt in range(2)]
        z_bf = sb("z_bf", [P, V * PACK], BF16)
        z_codes = sb("z_codes", [P, V], U32)
        z_scales = sb("z_scales", [P, V], U8)
        def piece(flat, x):
            return flat.rearrange("p (bank x c) -> p bank x c", bank=2, x=2)[:, :, x, :]

        for vt in range(2):
            factors = (paq_w[vt][:].rearrange("p v t -> p (v t)"), half_z[vt][:])
            products = (half_z[vt][:], z_bf[:, P * PACK * vt : P * PACK * (vt + 1)])
            for d in range(2):
                for x in range(2):
                    nc.vector.scalar_tensor_tensor(
                        out=piece(products[d], x), in0=piece(uncovered[vt][:, d].rearrange("p v t -> p (v t)"), x), scalar=0.001,
                        in1=piece(factors[d], x), op0=ADD, op1=MULT,
                    )

        out_view = out.rearrange("(vt p) j -> p vt j", p=P)
        dd_bf = [sb("dd_bf%d" % c, [P, n, PACK], BF16) for c, (j0, n) in enumerate(CAND_CHUNKS)]

        covered = [sb("covered%d" % hf, [P, PACK, 256], F32) for hf in range(2)]
        for hf in range(2):
            for t in range(PACK):
                nc.scalar.activation(out=covered[hf][:, t, :], in_=cand_acc[t][:, 256 * hf : 256 * (hf + 1)], func=SIGMOID)

        def make_dd(c):
            j0, n = CAND_CHUNKS[c]
            values = covered[j0 // 256][:, :, j0 % 256 : j0 % 256 + n]
            dst = dd_bf[c][:].rearrange("p (c i) t -> p c t i", i=4)
            if c == len(CAND_CHUNKS) - 1:
                planes = sb("planes", [P, PACK, n], BF16, tag="planes")
                for t in range(PACK):
                    nc.scalar.activation(out=planes[:, t, :], in_=values[:, t, :], func=COPY, scale=unit_t[:, t : t + 1])
                nc.scalar.copy(out=dst, in_=planes[:].rearrange("p t (c i) -> p c t i", i=4))
            else:
                nc.vector.tensor_tensor(
                    out=dst,
                    in0=values.rearrange("p t (c i) -> p c t i", i=4),
                    in1=unit_t.unsqueeze(1).unsqueeze(3).to_broadcast([P, n // 4, PACK, 4]),
                    op=MULT,
                )

        def score(c):
            j0, n = CAND_CHUNKS[c]
            dd_codes = sb("dd_codes%d" % c, [P, n], U32)
            dd_scales = sb("dd_scales%d" % c, [P, n], U8)
            quantize(dd_codes[:], dd_scales[:], dd_bf[c][:].rearrange("p j t -> p (j t)"))
            acc = psum.tile([P, 2, n], F32, name="scores", tag="narrow", bufs=4)
            for vt in range(2):
                nc.tensor.matmul_mx(
                    out=acc[:, vt, :],
                    lhsT=z_codes[:, P * vt : P * (vt + 1)].bitcast(FP8X4), lhsT_scale=z_scales[:, P * vt : P * (vt + 1)],
                    rhs=dd_codes[:].bitcast(FP8X4), rhs_scale=dd_scales[:],
                    start=True, stop=True,
                )
            result = sb("result%d" % c, [P, 2, n], F32, tag="planes" if c == 0 else "")
            if c == 1:
                nc.vector.tensor_copy(out=result[:], in_=acc[:])
            else:
                nc.scalar.copy(out=result[:], in_=acc[:])
            nc.sync.dma_start(out=out_view[:, :, j0 : j0 + n], in_=result[:])

        make_dd(0)
        make_dd(2)
        quantize(z_codes[:], z_scales[:], z_bf[:])
        score(0)
        make_dd(1)
        score(1)
        score(2)
